import numpy as np
import ml_dtypes


def mxq(x, axis, fmt="e4m3"):
    dtype, down = {"e4m3": (ml_dtypes.float8_e4m3fn, 7), "e5m2": (ml_dtypes.float8_e5m2, 14)}[fmt]
    v = np.moveaxis(np.asarray(x, np.float32).astype(ml_dtypes.bfloat16).astype(np.float64), axis, -1)
    blocks = v.reshape(v.shape[:-1] + (-1, 32))
    amax = np.abs(blocks).max(-1, keepdims=True)
    byte = np.maximum(np.where(amax > 0, np.frexp(amax)[1] - 1 + 127, 0) - down, 1)
    scale = np.exp2(byte - 127.0)
    codes = (blocks / scale).astype(np.float32).astype(dtype).astype(np.float64)
    return np.moveaxis((codes * scale).reshape(v.shape), -1, axis)


WIDE = False


def mx_kscale(k):
    if not WIDE:
        return np.ones(k)
    levels = np.array([10, -10, 5, -5, 0])
    if k % 512:
        return np.exp2(np.random.permutation(np.resize(levels, k // 32))).repeat(32)
    a = np.empty((k // 512, 16))
    for p in range(k // 512):
        a[p, :8] = np.random.permutation(np.resize(levels, 8))
        for g in range(8):
            far = levels[np.abs(levels - a[p, g]) >= 10]
            a[p, g + 8] = far[np.random.randint(len(far))]
    return np.exp2(a.ravel()).repeat(32)


def f64(x):
    return np.asarray(x).astype(np.float64)


def striped(idx):
    return np.tile(np.asarray(idx).reshape(-1, 16).T, (8, 1)).astype(np.uint16)


def unstriped(offs):
    return offs[:16].T.reshape(-1).astype(np.int64)


def striped8(idx):
    return np.asarray(idx).reshape(8, -1, 16).transpose(0, 2, 1).reshape(128, -1).astype(np.uint16)


def unstriped8(offs):
    return offs.reshape(8, 16, -1).transpose(0, 2, 1).reshape(8, -1).astype(np.int64)


def pick8(x, idx, run):
    r = np.arange(len(x))
    return x[r[:, None], idx[r % (8 * run) // run]]


E2M1 = np.array([0.0, 0.5, 1.0, 1.5, 2.0, 3.0, 4.0, 6.0, -0.0, -0.5, -1.0, -1.5, -2.0, -3.0, -4.0, -6.0])


def pack_weight(w, fmt):
    k, n = w.shape
    w = f64(np.asarray(w, np.float32).astype(ml_dtypes.bfloat16)).reshape(k // 32, 32, n)
    amax = np.abs(w).max(1)
    if fmt == "e4m3":
        byte = np.frexp(amax)[1] - 1 + 127 - 7
    else:
        mant, ex = np.frexp(amax / 6.0)
        byte = np.where(mant > 0.5, ex, ex - 1) + 127
    byte = np.clip(np.where(amax > 0, byte, 1), 1, 254)
    scaled = (w * np.exp2(127.0 - byte)[:, None, :]).reshape(k, n).astype(np.float32)
    by_word = np.ascontiguousarray(scaled.reshape(k // 512, 128, 4, n).transpose(0, 1, 3, 2))
    if fmt == "e4m3":
        words = by_word.astype(ml_dtypes.float8_e4m3fn).view(np.uint8)
    else:
        c = by_word.astype(ml_dtypes.float4_e2m1fn).view(np.uint8) & 0xF
        words = (c[..., 0::2] | (c[..., 1::2] << 4)).reshape(k // 512, 128, 2 * n)
    return np.ascontiguousarray(words), np.ascontiguousarray(byte.astype(np.uint8).reshape(k // 512, 16, n))


def unpack_weight(words, scales, fmt):
    g, _, n = scales.shape
    words = np.ascontiguousarray(words).reshape(g, 128, n, -1)
    if fmt == "e4m3":
        vals = words.view(ml_dtypes.float8_e4m3fn).astype(np.float64)
    else:
        nib = np.empty((g, 128, n, 4), np.uint8)
        nib[..., 0::2] = words & 0xF
        nib[..., 1::2] = words >> 4
        vals = E2M1[nib]
    vals = vals * np.repeat(np.exp2(scales.astype(np.float64) - 127.0), 8, axis=1)[..., None]
    return vals.transpose(0, 1, 3, 2).reshape(g * 512, n)


K, J, R, T, U, Z, M, O, C, N, S = 512, 256, 512, 1024, 512, 512, 1024, 128, 512, 256, 1024


def setup_inputs():
    n = np.random.standard_normal
    idx = np.stack([np.random.permutation(T)[:U] for _ in range(8)])
    idx2 = np.random.permutation(U)[:J]
    idx3 = np.random.permutation(M)[:J]
    idx4 = np.stack([np.random.permutation(C)[:J] for _ in range(8)])
    idx5 = np.stack([np.random.permutation(C)[:O] for _ in range(8)])
    idx6 = np.stack([np.random.permutation(J)[:O] for _ in range(8)])
    idx7 = np.random.permutation(S)[:N]
    fk = mx_kscale(K)
    fr = mx_kscale(R)
    fz = mx_kscale(Z)
    wp = pack_weight(n((K, R)) * 1 / np.sqrt(K) / fk[:, None] * fr, "e4m3")
    xop = pack_weight(n((Z, M)) / fz[:, None], "e4m3")
    w2p = pack_weight(n((Z, R)) * 1 / np.sqrt(Z) * fz[:, None] * fr, "e2m1")
    vsp = pack_weight(n((R, S)) * 1 / np.sqrt(R) / fr[:, None], "e2m1")
    return {
        "ta": (np.random.randint(-7, 8, (K, T)).astype(np.float64)).astype(np.float32),
        "ga": ((np.random.randint(8, 25, (K, 1)) / 64.0) * fk[:, None]).astype(np.float32),
        "gb": (np.random.uniform(0.5, 1.6, (K, 1))).astype(np.float32),
        "w_words": wp[0],
        "w_scales": wp[1],
        "xo_words": xop[0],
        "xo_scales": xop[1],
        "w2_words": w2p[0],
        "w2_scales": w2p[1],
        "sa": (np.random.uniform(0.5, 1.6, (R, 1))).astype(np.float32),
        "sb": (np.random.uniform(0.5, 1.6, (R, 1))).astype(np.float32),
        "vs_words": vsp[0],
        "vs_scales": vsp[1],
        "offs": striped8(idx),
        "offs2": striped(idx2),
        "offs3": striped(idx3),
        "offs4": striped8(idx4),
        "offs5": striped8(idx5),
        "offs6": striped8(idx6),
        "offs7": striped(idx7),
    }


def reference(ta, ga, gb, w_words, w_scales, xo_words, xo_scales, w2_words, w2_scales, sa, sb, vs_words, vs_scales, offs, offs2, offs3, offs4, offs5, offs6, offs7):
    idx = unstriped8(offs)
    idx2 = unstriped(offs2)
    idx3 = unstriped(offs3)
    idx4 = unstriped8(offs4)
    idx5 = unstriped8(offs5)
    idx6 = unstriped8(offs6)
    idx7 = unstriped(offs7)
    wu = unpack_weight(w_words, w_scales, "e4m3")
    xou = unpack_weight(xo_words, xo_scales, "e4m3")
    w2u = unpack_weight(w2_words, w2_scales, "e2m1")
    vsu = unpack_weight(vs_words, vs_scales, "e2m1")
    xcd = pick8(f64(ta), idx, 64) * f64(ga)
    xc = xcd[:, idx2] * f64(gb)
    xcq = mxq(xc, 0, "e4m3")
    a = wu.T @ xcq
    xoidx3g = xou[:, idx3]
    b = w2u.T @ xoidx3g
    pw = np.zeros((R, C))
    pw[np.arange(R)[:, None], idx4[np.arange(R) % 512 // 64]] = a
    hid = np.maximum(pick8(pw, idx5, 64) * f64(sa), pick8(b, idx6, 64) * f64(sb))
    vsidx7g = vsu[:, idx7]
    hidq = mxq(hid, 0, "e4m3")
    y = vsidx7g.T @ hidq
    return y

@@ -1,0 +1,269 @@
+from contextlib import ExitStack
+
+import concourse.mybir as mybir
+
+K, J, R, T, U, Z, M, O, C, N, S = 512, 256, 512, 1024, 512, 512, 1024, 128, 512, 256, 1024
+FLOPS = 2 * K * R * J + 2 * Z * R * J + 2 * R * N * O
+
+F32 = mybir.dt.float32
+BF16 = mybir.dt.bfloat16
+I32 = mybir.dt.int32
+U32 = mybir.dt.uint32
+U16 = mybir.dt.uint16
+U8 = mybir.dt.uint8
+FP8X4 = mybir.dt.float8_e4m3fn_x4
+FP4X4 = mybir.dt.float4_e2m1fn_x4
+COPY = mybir.ActivationFunctionType.Copy
+MAX = mybir.AluOpType.max
+
+P = 128
+PACK = 4
+QUADS = 4
+HALF = J // 2
+LIST_ROWS = 16
+
+
+def tile_picked_respelled_plain_two_boardmeet_store_plain_kernel(
+    tc, ta, ga, gb, w_words, w_scales, xo_words, xo_scales, w2_words, w2_scales, sa, sb,
+    vs_words, vs_scales, offs, offs2, offs3, offs4, offs5, offs6, offs7, out,
+):
+    nc = tc.nc
+    with ExitStack() as ctx:
+        lists = ctx.enter_context(tc.tile_pool(name="lists", bufs=1))
+        keep = ctx.enter_context(tc.tile_pool(name="keep", bufs=1))
+        reuse = ctx.enter_context(tc.tile_pool(name="reuse", bufs=1))
+        psum = ctx.enter_context(tc.psum_pool(name="psum", bufs=1))
+
+        def load_list(source, name):
+            tile = lists.tile(list(source.shape), U16, name=name)
+            nc.sync.dma_start(tile[:], source)
+            return tile
+
+        def load_column(queue, source, name):
+            tile = keep.tile([P, PACK], F32, name=name, tag=name, align_bytes=64)
+            queue.dma_start(out=tile[:], in_=source.rearrange("(p t) one -> p (t one)", t=PACK))
+            return tile
+
+        def load_table_rows(t):
+            tile = keep.tile([P, T], F32, name="ta%d" % t, tag="ta%d" % t, align_bytes=64)
+            nc.sync.dma_start(out=tile[:], in_=ta.rearrange("(p t) c -> p t c", t=PACK)[:, t, :])
+            return tile
+
+        def load_bytes(source, name):
+            tile = keep.tile([P, source.shape[1] // 4], I32, name=name, tag=name, align_bytes=64)
+            nc.sync.dma_start(out=tile[:], in_=source.bitcast(I32))
+            return tile
+
+        def staging(width, first, name):
+            tile = keep.tile([P, QUADS, width // 4], I32, name=name)
+            nc.vector.memset(tile[first : first + 32, :, :], 0)
+            return tile
+
+        def load_scale_rows(staged, first, source):
+            rows = source[0].rearrange("(q r) c -> r q c", r=PACK)
+            nc.sync.dma_start(out=staged[first : first + PACK, :, :], in_=rows.bitcast(I32))
+
+        def spread(staged, first, name):
+            plane = keep.tile([P, 4 * staged.shape[2]], U8, name=name, align_bytes=64)
+            for q in range(QUADS):
+                nc.vector.tensor_copy(
+                    out=plane[32 * q : 32 * (q + 1), :].bitcast(I32), in_=staged[first : first + 32, q, :]
+                )
+            return plane
+
+        def deal(engine_copy, dealt, raw):
+            engine_copy(
+                out=dealt.rearrange("p (t c i) -> p c t i", t=PACK, i=4),
+                in_=raw.rearrange("p (c i t) -> p c t i", t=PACK, i=4),
+            )
+
+        weight_rows = staging(R, 64, "weight_rows")
+        vs_rows = keep.tile([P, 2, S // 4], I32, name="vs_rows")
+        vs_plane = keep.tile([P, S], U8, name="vs_plane", align_bytes=64)
+        nc.vector.memset(vs_plane[:].bitcast(I32), 0)
+        xo_rows = keep.tile([PACK, QUADS, M // 4], I32, name="xo_rows")
+        xo_plane = keep.tile([P, M], U8, name="xo_plane", align_bytes=64)
+        nc.vector.memset(xo_plane[:].bitcast(I32), 0)
+
+        idx = load_list(offs, "idx")
+        ga_sb = load_column(nc.scalar, ga, "ga_sb")
+        ta_sb = [load_table_rows(0)]
+        gb_sb = load_column(nc.scalar, gb, "gb_sb")
+        idx2 = load_list(offs2, "idx2")
+        ta_sb.append(load_table_rows(1))
+        load_scale_rows(xo_rows, 0, xo_scales)
+        idx3 = load_list(offs3, "idx3")
+        vs_halves = vs_scales[0].rearrange("(u q r) c -> u r q c", u=2, r=PACK)
+        nc.sync.dma_start(out=vs_rows[0:PACK, :, :], in_=vs_halves[0].bitcast(I32))
+        ta_sb.append(load_table_rows(2))
+        nc.sync.dma_start(out=vs_rows[64 : 64 + PACK, :, :], in_=vs_halves[1].bitcast(I32))
+        idx7 = load_list(offs7, "idx7")
+        ta_sb.append(load_table_rows(3))
+        load_scale_rows(weight_rows, 64 + PACK, w_scales)
+        load_scale_rows(weight_rows, 64, w2_scales)
+        w_raw = load_bytes(w_words[0].rearrange("p n t -> p (n t)"), "w_raw")
+        w2_raw = load_bytes(w2_words[0], "w2_raw")
+        xo_raw = reuse.tile([P, M], I32, name="xo_raw", offset=0, align_bytes=64)
+        nc.sync.dma_start(out=xo_raw[:], in_=xo_words[0].rearrange("p n t -> p (n t)").bitcast(I32))
+        idx4 = load_list(offs4, "idx4")
+        vs_raw = load_bytes(vs_words[0], "vs_raw")
+        idx6 = load_list(offs6, "idx6")
+        sb_sb = load_column(nc.sync, sb, "sb_sb")
+        idx5 = load_list(offs5, "idx5")
+        sa_sb = load_column(nc.sync, sa, "sa_sb")
+
+        board = [keep.tile([P, C], F32, name="board%d" % t) for t in range(PACK)]
+        for t in range(PACK):
+            nc.vector.memset(board[t][:], 0.0)
+
+        xcd = [keep.tile([P, U], F32, name="xcd%d" % t) for t in range(PACK)]
+
+        def spell_words(t):
+            nc.scalar.activation(out=xcd[t][:], in_=ta_sb[t][:].indirect(idx[:]), func=COPY, scale=ga_sb[:, t : t + 1])
+
+        def read_slots(h, t, target):
+            columns = slice(h * HALF // LIST_ROWS, (h + 1) * HALF // LIST_ROWS)
+            nc.scalar.activation(
+                out=target, in_=xcd[t][:].indirect(idx2[:, columns]), func=COPY, scale=gb_sb[:, t : t + 1]
+            )
+
+        def weave(engine_copy, woven, planes):
+            engine_copy(
+                out=woven.rearrange("p (c i) t -> p c t i", i=4), in_=planes.rearrange("p t (c i) -> p c t i", i=4)
+            )
+
+        pairs = []
+        for pair in range(2):
+            spell_words(2 * pair)
+            spell_words(2 * pair + 1)
+            planes = keep.tile([P, 2, HALF], BF16, name="xc0_%d" % pair, tag="ta%d" % (2 * pair + 1), align_bytes=64)
+            for i in range(2):
+                read_slots(0, 2 * pair + i, planes[:, i, :])
+            pairs.append(planes)
+
+        for q in range(QUADS):
+            nc.vector.tensor_copy(out=xo_plane[32 * q : 32 * q + PACK, :].bitcast(I32), in_=xo_rows[:, q, :])
+        xo_scale = keep.tile([P, J], U8, name="xo_scale", align_bytes=64)
+        nc.vector.tensor_copy(out=xo_scale[:], in_=xo_plane[:].indirect(idx3[:]))
+        woven = keep.tile([P, HALF, PACK], BF16, name="xc_woven0", align_bytes=64)
+        weave(nc.vector.tensor_copy, woven[:, :, 0:2], pairs[0][:])
+        for q in range(QUADS):
+            first = 64 * (q // 2)
+            nc.vector.tensor_copy(
+                out=vs_plane[32 * q : 32 * q + PACK, :].bitcast(I32), in_=vs_rows[first : first + PACK, q % 2, :]
+            )
+        vs_scale = keep.tile([P, N], U8, name="vs_scale", align_bytes=64)
+        nc.vector.tensor_copy(out=vs_scale[:], in_=vs_plane[:].indirect(idx7[:]))
+        weight_plane = spread(weight_rows, 64, "weight_plane")
+        weight_scale = keep.tile([P, R], U8, name="weight_scale", align_bytes=64)
+        deal(nc.vector.tensor_copy, weight_scale[:], weight_plane[:])
+        w_codes = keep.tile([P, R], I32, name="w_codes", align_bytes=64)
+        deal(nc.vector.tensor_copy, w_codes[:], w_raw[:])
+
+        def shared(shape, dtype, name, tag):
+            if tag == "a_first":
+                return reuse.tile(shape, dtype, name=name, tag=tag, offset=1024, align_bytes=64)
+            return keep.tile(shape, dtype, name=name, tag=tag, align_bytes=64)
+
+        def quantize_slots(h, woven, tag):
+            codes = shared([P, HALF], U32, "xc_codes%d" % h, tag)
+            scale = keep.tile([P, HALF], U8, name="xc_scale%d" % h, tag="xc_scale%d" % h, align_bytes=64)
+            nc.vector.quantize_mx(
+                out=codes[:].bitcast(FP8X4), scales=scale[:], in_=woven[:].rearrange("p j t -> p (j t)")
+            )
+            return codes, scale
+
+        def first_product(h, codes, scale, tiles):
+            bank = psum.tile([P, len(tiles), HALF], F32, name="a_bank%d_%d" % (h, tiles[0]), tag="a_bank%d_%d" % (h, tiles[0]))
+            for i, t in enumerate(tiles):
+                rows = slice(t * P, (t + 1) * P)
+                nc.tensor.matmul_mx(
+                    out=bank[:, i, :], lhsT=w_codes[:, rows].bitcast(FP8X4), lhsT_scale=weight_scale[PACK:, rows],
+                    rhs=codes[:].bitcast(FP8X4), rhs_scale=scale[:], start=True, stop=True,
+                )
+            return bank
+
+        a_sb = {}
+
+        def empty_bank(h, bank, tiles, tag):
+            tile = shared([P, len(tiles), HALF], F32, "a_sb%d_%d" % (h, tiles[0]), tag)
+            nc.scalar.copy(out=tile[:], in_=bank[:])
+            for i, t in enumerate(tiles):
+                a_sb[h, t] = tile[:, i, :]
+
+        def put_on_board(h, t):
+            columns = slice(h * HALF // LIST_ROWS, (h + 1) * HALF // LIST_ROWS)
+            nc.vector.tensor_copy(out=board[t][:].indirect(idx4[:, columns]), in_=a_sb[h, t])
+
+        weave(nc.vector.tensor_copy, woven[:, :, 2:4], pairs[1][:])
+        codes, scale = quantize_slots(0, woven, "xc_codes0")
+        planes = keep.tile([P, PACK, HALF], BF16, name="xc1", tag="ga_sb", align_bytes=64)
+        for t in range(PACK):
+            read_slots(1, t, planes[:, t, :])
+        first_bank = first_product(0, codes, scale, [0])
+        rest_bank = first_product(0, codes, scale, [1, 2, 3])
+        xo_codes = keep.tile([P, J], U32, name="xo_codes", align_bytes=64)
+        nc.vector.tensor_copy(out=xo_codes[:], in_=xo_raw[:].bitcast(U32).indirect(idx3[:]))
+        woven = reuse.tile([P, HALF, PACK], BF16, name="xc_woven1", offset=0, align_bytes=64)
+        for pair in range(2):
+            weave(nc.vector.tensor_copy, woven[:, :, 2 * pair : 2 * pair + 2], planes[:, 2 * pair : 2 * pair + 2, :])
+        empty_bank(0, first_bank, [0], "a_first")
+        w2_codes = reuse.tile([P, 2 * R], U8, name="w2_codes", offset=2048, align_bytes=64)
+        deal(nc.scalar.copy, w2_codes[:].bitcast(U16), w2_raw[:].bitcast(U16))
+        empty_bank(0, rest_bank, [1, 2, 3], "w2_raw")
+        put_on_board(0, 0)
+        codes, scale = quantize_slots(1, woven, "a_first")
+        for t in range(1, PACK):
+            put_on_board(0, t)
+        empty_bank(1, first_product(1, codes, scale, [0, 1, 2, 3]), [0, 1, 2, 3], "a_second")
+
+        b_tags = ("a_first", "xc_scale1", "b_sb2", "b_sb3")
+        b_sb = [shared([P, J], F32, "b_sb%d" % t, b_tags[t]) for t in range(PACK)]
+        from_b = keep.tile([P, PACK, O], F32, name="from_b")
+        for pair in range(2):
+            bank = psum.tile([P, 2, J], F32, name="b_bank%d" % pair, tag=("b_bank0", "a_bank1_0")[pair])
+            for i in range(2):
+                t = 2 * pair + i
+                nc.tensor.matmul_mx(
+                    out=bank[:, i, :], lhsT=w2_codes[:, 2 * t * P : 2 * (t + 1) * P].bitcast(FP4X4),
+                    lhsT_scale=weight_scale[:, t * P : (t + 1) * P],
+                    rhs=xo_codes[:].bitcast(FP8X4), rhs_scale=xo_scale[:], start=True, stop=True,
+                )
+            for i in range(2):
+                nc.scalar.copy(out=b_sb[2 * pair + i][:], in_=bank[:, i, :])
+        for t in range(PACK):
+            nc.scalar.activation(
+                out=from_b[:, t, :], in_=b_sb[t][:].indirect(idx6[:]), func=COPY, scale=sb_sb[:, t : t + 1]
+            )
+
+        from_board = keep.tile([P, PACK, O], F32, name="from_board")
+        for t in range(PACK):
+            put_on_board(1, t)
+            nc.scalar.activation(
+                out=from_board[:, t, :], in_=board[t][:].indirect(idx5[:]), func=COPY, scale=sa_sb[:, t : t + 1]
+            )
+
+        vs_codes = keep.tile([P, 2 * N], U8, name="vs_codes", tag="a_second", align_bytes=64)
+        nc.vector.tensor_copy(out=vs_codes[:].bitcast(U16), in_=vs_raw[:].bitcast(U16).indirect(idx7[:]))
+        hid = keep.tile([P, O, PACK], BF16, name="hid", align_bytes=64)
+        nc.vector.tensor_tensor(
+            out=hid[:].rearrange("p (c i) t -> p c t i", i=4),
+            in0=from_board[:].rearrange("p t (c i) -> p c t i", i=4),
+            in1=from_b[:].rearrange("p t (c i) -> p c t i", i=4),
+            op=MAX,
+        )
+        hid_codes = keep.tile([P, O], U32, name="hid_codes", align_bytes=64)
+        hid_scale = keep.tile([P, O], U8, name="hid_scale", align_bytes=64)
+        nc.vector.quantize_mx(
+            out=hid_codes[:].bitcast(FP8X4), scales=hid_scale[:], in_=hid[:].rearrange("p o t -> p (o t)")
+        )
+        for h, (engine_copy, queue) in enumerate(((nc.scalar.copy, nc.scalar), (nc.vector.tensor_copy, nc.sync))):
+            bank = psum.tile([P, O], F32, name="y_bank%d" % h)
+            nc.tensor.matmul_mx(
+                out=bank[:], lhsT=vs_codes[:, 2 * h * P : 2 * (h + 1) * P].bitcast(FP4X4),
+                lhsT_scale=vs_scale[:, h * P : (h + 1) * P],
+                rhs=hid_codes[:].bitcast(FP8X4), rhs_scale=hid_scale[:], start=True, stop=True,
+            )
+            result = keep.tile([P, O], F32, name="result%d" % h)
+            engine_copy(out=result[:], in_=bank[:])
+            queue.dma_start(out=out[h * P : (h + 1) * P, :], in_=result[:])

@@ -77,6 +77,10 @@ def tile_picked_respelled_plain_two_boardmeet_store_plain_kernel(
                 in_=raw.rearrange("p (c i t) -> p c t i", t=PACK, i=4),
             )
 
+        warm_in = keep.tile([P, 1], F32, name="warm_in")
+        warm_out = keep.tile([P, 1], F32, name="warm_out")
+        nc.gpsimd.memset(warm_in[:], 0.0)
+        nc.scalar.activation(out=warm_out[:], in_=warm_in[:], func=COPY)
         weight_rows = staging(R, 64, "weight_rows")
         vs_rows = keep.tile([P, 2, S // 4], I32, name="vs_rows")
         vs_plane = keep.tile([P, S], U8, name="vs_plane", align_bytes=64)

@@ -59,9 +59,9 @@ def tile_picked_respelled_plain_two_boardmeet_store_plain_kernel(
             nc.vector.memset(tile[first : first + 32, :, :], 0)
             return tile
 
-        def load_scale_rows(staged, first, source):
+        def load_scale_rows(queue, staged, first, source):
             rows = source[0].rearrange("(q r) c -> r q c", r=PACK)
-            nc.sync.dma_start(out=staged[first : first + PACK, :, :], in_=rows.bitcast(I32))
+            queue.dma_start(out=staged[first : first + PACK, :, :], in_=rows.bitcast(I32))
 
         def spread(staged, first, name):
             plane = keep.tile([P, 4 * staged.shape[2]], U8, name=name, align_bytes=64)
@@ -93,22 +93,22 @@ def tile_picked_respelled_plain_two_boardmeet_store_plain_kernel(
         ga_sb = load_column(nc.scalar, ga, "ga_sb")
         ta_sb = [load_table_rows(0)]
         gb_sb = load_column(nc.scalar, gb, "gb_sb")
-        idx2 = load_list(offs2, "idx2")
         ta_sb.append(load_table_rows(1))
-        load_scale_rows(xo_rows, 0, xo_scales)
-        idx3 = load_list(offs3, "idx3")
-        vs_halves = vs_scales[0].rearrange("(u q r) c -> u r q c", u=2, r=PACK)
-        nc.sync.dma_start(out=vs_rows[0:PACK, :, :], in_=vs_halves[0].bitcast(I32))
+        idx2 = load_list(offs2, "idx2")
+        load_scale_rows(nc.scalar, weight_rows, 64 + PACK, w_scales)
+        load_scale_rows(nc.scalar, weight_rows, 64, w2_scales)
         ta_sb.append(load_table_rows(2))
-        nc.sync.dma_start(out=vs_rows[64 : 64 + PACK, :, :], in_=vs_halves[1].bitcast(I32))
-        idx7 = load_list(offs7, "idx7")
+        load_scale_rows(nc.sync, xo_rows, 0, xo_scales)
+        idx3 = load_list(offs3, "idx3")
         ta_sb.append(load_table_rows(3))
-        load_scale_rows(weight_rows, 64 + PACK, w_scales)
-        load_scale_rows(weight_rows, 64, w2_scales)
+        vs_halves = vs_scales[0].rearrange("(u q r) c -> u r q c", u=2, r=PACK)
+        nc.sync.dma_start(out=vs_rows[64 : 64 + PACK, :, :], in_=vs_halves[1].bitcast(I32))
+        nc.sync.dma_start(out=vs_rows[0:PACK, :, :], in_=vs_halves[0].bitcast(I32))
+        idx7 = load_list(offs7, "idx7")
         w_raw = load_bytes(w_words[0].rearrange("p n t -> p (n t)"), "w_raw")
-        w2_raw = load_bytes(w2_words[0], "w2_raw")
         xo_raw = reuse.tile([P, M], I32, name="xo_raw", offset=0, align_bytes=64)
         nc.sync.dma_start(out=xo_raw[:], in_=xo_words[0].rearrange("p n t -> p (n t)").bitcast(I32))
+        w2_raw = load_bytes(w2_words[0], "w2_raw")
         idx4 = load_list(offs4, "idx4")
         vs_raw = load_bytes(vs_words[0], "vs_raw")
         idx6 = load_list(offs6, "idx6")
@@ -136,21 +136,24 @@ def tile_picked_respelled_plain_two_boardmeet_store_plain_kernel(
                 out=woven.rearrange("p (c i) t -> p c t i", i=4), in_=planes.rearrange("p t (c i) -> p c t i", i=4)
             )
 
-        pairs = []
-        for pair in range(2):
-            spell_words(2 * pair)
-            spell_words(2 * pair + 1)
-            planes = keep.tile([P, 2, HALF], BF16, name="xc0_%d" % pair, tag="ta%d" % (2 * pair + 1), align_bytes=64)
-            for i in range(2):
-                read_slots(0, 2 * pair + i, planes[:, i, :])
-            pairs.append(planes)
+        planes = keep.tile([P, PACK, HALF], BF16, name="xc0", align_bytes=64)
+        spell_words(0)
+        spell_words(1)
+        read_slots(0, 0, planes[:, 0, :])
+        read_slots(0, 1, planes[:, 1, :])
+        for t in range(2, PACK):
+            spell_words(t)
+            read_slots(0, t, planes[:, t, :])
 
+        weight_plane = spread(weight_rows, 64, "weight_plane")
+        weight_scale = keep.tile([P, R], U8, name="weight_scale", align_bytes=64)
+        deal(nc.vector.tensor_copy, weight_scale[:], weight_plane[:])
         for q in range(QUADS):
             nc.vector.tensor_copy(out=xo_plane[32 * q : 32 * q + PACK, :].bitcast(I32), in_=xo_rows[:, q, :])
         xo_scale = keep.tile([P, J], U8, name="xo_scale", align_bytes=64)
         nc.vector.tensor_copy(out=xo_scale[:], in_=xo_plane[:].indirect(idx3[:]))
         woven = keep.tile([P, HALF, PACK], BF16, name="xc_woven0", align_bytes=64)
-        weave(nc.vector.tensor_copy, woven[:, :, 0:2], pairs[0][:])
+        weave(nc.vector.tensor_copy, woven[:, :, 0:2], planes[:, 0:2, :])
         for q in range(QUADS):
             first = 64 * (q // 2)
             nc.vector.tensor_copy(
@@ -158,9 +161,6 @@ def tile_picked_respelled_plain_two_boardmeet_store_plain_kernel(
             )
         vs_scale = keep.tile([P, N], U8, name="vs_scale", align_bytes=64)
         nc.vector.tensor_copy(out=vs_scale[:], in_=vs_plane[:].indirect(idx7[:]))
-        weight_plane = spread(weight_rows, 64, "weight_plane")
-        weight_scale = keep.tile([P, R], U8, name="weight_scale", align_bytes=64)
-        deal(nc.vector.tensor_copy, weight_scale[:], weight_plane[:])
         w_codes = keep.tile([P, R], I32, name="w_codes", align_bytes=64)
         deal(nc.vector.tensor_copy, w_codes[:], w_raw[:])
 
@@ -199,7 +199,7 @@ def tile_picked_respelled_plain_two_boardmeet_store_plain_kernel(
             columns = slice(h * HALF // LIST_ROWS, (h + 1) * HALF // LIST_ROWS)
             nc.vector.tensor_copy(out=board[t][:].indirect(idx4[:, columns]), in_=a_sb[h, t])
 
-        weave(nc.vector.tensor_copy, woven[:, :, 2:4], pairs[1][:])
+        weave(nc.vector.tensor_copy, woven[:, :, 2:4], planes[:, 2:4, :])
         codes, scale = quantize_slots(0, woven, "xc_codes0")
         planes = keep.tile([P, PACK, HALF], BF16, name="xc1", tag="ga_sb", align_bytes=64)
         for t in range(PACK):

@@ -71,10 +71,10 @@ def tile_picked_respelled_plain_two_boardmeet_store_plain_kernel(
                 )
             return plane
 
-        def deal(engine_copy, dealt, raw):
+        def deal(engine_copy, dealt, raw, run):
             engine_copy(
-                out=dealt.rearrange("p (t c i) -> p c t i", t=PACK, i=4),
-                in_=raw.rearrange("p (c i t) -> p c t i", t=PACK, i=4),
+                out=dealt.rearrange("p (t c i) -> p c t i", t=PACK, i=run),
+                in_=raw.rearrange("p (c i t) -> p c t i", t=PACK, i=run),
             )
 
         warm_in = keep.tile([P, 1], F32, name="warm_in")
@@ -147,13 +147,11 @@ def tile_picked_respelled_plain_two_boardmeet_store_plain_kernel(
 
         weight_plane = spread(weight_rows, 64, "weight_plane")
         weight_scale = keep.tile([P, R], U8, name="weight_scale", align_bytes=64)
-        deal(nc.vector.tensor_copy, weight_scale[:], weight_plane[:])
+        deal(nc.vector.tensor_copy, weight_scale[:], weight_plane[:], 16)
         for q in range(QUADS):
             nc.vector.tensor_copy(out=xo_plane[32 * q : 32 * q + PACK, :].bitcast(I32), in_=xo_rows[:, q, :])
         xo_scale = keep.tile([P, J], U8, name="xo_scale", align_bytes=64)
         nc.vector.tensor_copy(out=xo_scale[:], in_=xo_plane[:].indirect(idx3[:]))
-        woven = keep.tile([P, HALF, PACK], BF16, name="xc_woven0", align_bytes=64)
-        weave(nc.vector.tensor_copy, woven[:, :, 0:2], planes[:, 0:2, :])
         for q in range(QUADS):
             first = 64 * (q // 2)
             nc.vector.tensor_copy(
@@ -162,7 +160,9 @@ def tile_picked_respelled_plain_two_boardmeet_store_plain_kernel(
         vs_scale = keep.tile([P, N], U8, name="vs_scale", align_bytes=64)
         nc.vector.tensor_copy(out=vs_scale[:], in_=vs_plane[:].indirect(idx7[:]))
         w_codes = keep.tile([P, R], I32, name="w_codes", align_bytes=64)
-        deal(nc.vector.tensor_copy, w_codes[:], w_raw[:])
+        deal(nc.vector.tensor_copy, w_codes[:], w_raw[:], 4)
+        woven = keep.tile([P, HALF, PACK], BF16, name="xc_woven0", tag="w_raw", align_bytes=64)
+        weave(nc.vector.tensor_copy, woven[:, :, 0:2], planes[:, 0:2, :])
 
         def shared(shape, dtype, name, tag):
             if tag == "a_first":
@@ -189,9 +189,10 @@ def tile_picked_respelled_plain_two_boardmeet_store_plain_kernel(
 
         a_sb = {}
 
-        def empty_bank(h, bank, tiles, tag):
+        def empty_bank(h, bank, tiles, tag, pieces):
             tile = shared([P, len(tiles), HALF], F32, "a_sb%d_%d" % (h, tiles[0]), tag)
-            nc.scalar.copy(out=tile[:], in_=bank[:])
+            for piece in pieces:
+                nc.scalar.copy(out=tile[:, piece, :], in_=bank[:, piece, :])
             for i, t in enumerate(tiles):
                 a_sb[h, t] = tile[:, i, :]
 
@@ -211,15 +212,15 @@ def tile_picked_respelled_plain_two_boardmeet_store_plain_kernel(
         woven = reuse.tile([P, HALF, PACK], BF16, name="xc_woven1", offset=0, align_bytes=64)
         for pair in range(2):
             weave(nc.vector.tensor_copy, woven[:, :, 2 * pair : 2 * pair + 2], planes[:, 2 * pair : 2 * pair + 2, :])
-        empty_bank(0, first_bank, [0], "a_first")
+        empty_bank(0, first_bank, [0], "a_first", [slice(0, 1)])
         w2_codes = reuse.tile([P, 2 * R], U8, name="w2_codes", offset=2048, align_bytes=64)
-        deal(nc.scalar.copy, w2_codes[:].bitcast(U16), w2_raw[:].bitcast(U16))
-        empty_bank(0, rest_bank, [1, 2, 3], "w2_raw")
+        deal(nc.scalar.copy, w2_codes[:].bitcast(U16), w2_raw[:].bitcast(U16), 8)
+        empty_bank(0, rest_bank, [1, 2, 3], "w2_raw", [slice(0, 1), slice(1, 3)])
         put_on_board(0, 0)
         codes, scale = quantize_slots(1, woven, "a_first")
         for t in range(1, PACK):
             put_on_board(0, t)
-        empty_bank(1, first_product(1, codes, scale, [0, 1, 2, 3]), [0, 1, 2, 3], "a_second")
+        empty_bank(1, first_product(1, codes, scale, [0, 1, 2, 3]), [0, 1, 2, 3], "a_second", [slice(0, 4)])
 
         b_tags = ("a_first", "xc_scale1", "b_sb2", "b_sb3")
         b_sb = [shared([P, J], F32, "b_sb%d" % t, b_tags[t]) for t in range(PACK)]

@@ -63,6 +63,16 @@ def tile_picked_respelled_plain_two_boardmeet_store_plain_kernel(
             rows = source[0].rearrange("(q r) c -> r q c", r=PACK)
             queue.dma_start(out=staged[first : first + PACK, :, :], in_=rows.bitcast(I32))
 
+        def zeroed_plane(width, name):
+            plane = keep.tile([P, width], U8, name=name, align_bytes=64)
+            nc.vector.memset(plane[:].bitcast(I32), 0)
+            return plane
+
+        def load_plane(plane, source):
+            rows = source[0].rearrange("(q r) c -> r q c", r=PACK)
+            for r in range(PACK):
+                nc.sync.dma_start(out=plane[r:P:32, :].bitcast(I32), in_=rows[r].bitcast(I32))
+
         def spread(staged, first, name):
             plane = keep.tile([P, 4 * staged.shape[2]], U8, name=name, align_bytes=64)
             for q in range(QUADS):
@@ -81,13 +91,9 @@ def tile_picked_respelled_plain_two_boardmeet_store_plain_kernel(
         warm_out = keep.tile([P, 1], F32, name="warm_out")
         nc.gpsimd.memset(warm_in[:], 0.0)
         nc.scalar.activation(out=warm_out[:], in_=warm_in[:], func=COPY)
+        xo_plane = zeroed_plane(M, "xo_plane")
         weight_rows = staging(R, 64, "weight_rows")
-        vs_rows = keep.tile([P, 2, S // 4], I32, name="vs_rows")
-        vs_plane = keep.tile([P, S], U8, name="vs_plane", align_bytes=64)
-        nc.vector.memset(vs_plane[:].bitcast(I32), 0)
-        xo_rows = keep.tile([PACK, QUADS, M // 4], I32, name="xo_rows")
-        xo_plane = keep.tile([P, M], U8, name="xo_plane", align_bytes=64)
-        nc.vector.memset(xo_plane[:].bitcast(I32), 0)
+        vs_plane = zeroed_plane(S, "vs_plane")
 
         idx = load_list(offs, "idx")
         ga_sb = load_column(nc.scalar, ga, "ga_sb")
@@ -98,14 +104,12 @@ def tile_picked_respelled_plain_two_boardmeet_store_plain_kernel(
         load_scale_rows(nc.scalar, weight_rows, 64 + PACK, w_scales)
         load_scale_rows(nc.scalar, weight_rows, 64, w2_scales)
         ta_sb.append(load_table_rows(2))
-        load_scale_rows(nc.sync, xo_rows, 0, xo_scales)
+        load_plane(xo_plane, xo_scales)
         idx3 = load_list(offs3, "idx3")
         ta_sb.append(load_table_rows(3))
-        vs_halves = vs_scales[0].rearrange("(u q r) c -> u r q c", u=2, r=PACK)
-        nc.sync.dma_start(out=vs_rows[64 : 64 + PACK, :, :], in_=vs_halves[1].bitcast(I32))
-        nc.sync.dma_start(out=vs_rows[0:PACK, :, :], in_=vs_halves[0].bitcast(I32))
-        idx7 = load_list(offs7, "idx7")
         w_raw = load_bytes(w_words[0].rearrange("p n t -> p (n t)"), "w_raw")
+        load_plane(vs_plane, vs_scales)
+        idx7 = load_list(offs7, "idx7")
         xo_raw = reuse.tile([P, M], I32, name="xo_raw", offset=0, align_bytes=64)
         nc.sync.dma_start(out=xo_raw[:], in_=xo_words[0].rearrange("p n t -> p (n t)").bitcast(I32))
         w2_raw = load_bytes(w2_words[0], "w2_raw")
@@ -148,21 +152,14 @@ def tile_picked_respelled_plain_two_boardmeet_store_plain_kernel(
         weight_plane = spread(weight_rows, 64, "weight_plane")
         weight_scale = keep.tile([P, R], U8, name="weight_scale", align_bytes=64)
         deal(nc.vector.tensor_copy, weight_scale[:], weight_plane[:], 16)
-        for q in range(QUADS):
-            nc.vector.tensor_copy(out=xo_plane[32 * q : 32 * q + PACK, :].bitcast(I32), in_=xo_rows[:, q, :])
         xo_scale = keep.tile([P, J], U8, name="xo_scale", align_bytes=64)
         nc.vector.tensor_copy(out=xo_scale[:], in_=xo_plane[:].indirect(idx3[:]))
-        for q in range(QUADS):
-            first = 64 * (q // 2)
-            nc.vector.tensor_copy(
-                out=vs_plane[32 * q : 32 * q + PACK, :].bitcast(I32), in_=vs_rows[first : first + PACK, q % 2, :]
-            )
-        vs_scale = keep.tile([P, N], U8, name="vs_scale", align_bytes=64)
-        nc.vector.tensor_copy(out=vs_scale[:], in_=vs_plane[:].indirect(idx7[:]))
+        woven = keep.tile([P, HALF, PACK], BF16, name="xc_woven0", align_bytes=64)
+        weave(nc.vector.tensor_copy, woven[:, :, 0:2], planes[:, 0:2, :])
         w_codes = keep.tile([P, R], I32, name="w_codes", align_bytes=64)
         deal(nc.vector.tensor_copy, w_codes[:], w_raw[:], 4)
-        woven = keep.tile([P, HALF, PACK], BF16, name="xc_woven0", tag="w_raw", align_bytes=64)
-        weave(nc.vector.tensor_copy, woven[:, :, 0:2], planes[:, 0:2, :])
+        vs_scale = keep.tile([P, N], U8, name="vs_scale", align_bytes=64)
+        nc.vector.tensor_copy(out=vs_scale[:], in_=vs_plane[:].indirect(idx7[:]))
 
         def shared(shape, dtype, name, tag):
             if tag == "a_first":

from contextlib import ExitStack

import concourse.mybir as mybir

K, J, R, T, U, Z, M, O, C, N, S = 512, 256, 512, 1024, 512, 512, 1024, 128, 512, 256, 1024
FLOPS = 2 * K * R * J + 2 * Z * R * J + 2 * R * N * O

F32 = mybir.dt.float32
BF16 = mybir.dt.bfloat16
I32 = mybir.dt.int32
U32 = mybir.dt.uint32
U16 = mybir.dt.uint16
U8 = mybir.dt.uint8
FP8X4 = mybir.dt.float8_e4m3fn_x4
FP4X4 = mybir.dt.float4_e2m1fn_x4
COPY = mybir.ActivationFunctionType.Copy
MAX = mybir.AluOpType.max

P = 128
PACK = 4
QUADS = 4
HALF = J // 2
LIST_ROWS = 16


def tile_picked_respelled_plain_two_boardmeet_store_plain_kernel(
    tc, ta, ga, gb, w_words, w_scales, xo_words, xo_scales, w2_words, w2_scales, sa, sb,
    vs_words, vs_scales, offs, offs2, offs3, offs4, offs5, offs6, offs7, out,
):
    nc = tc.nc
    with ExitStack() as ctx:
        lists = ctx.enter_context(tc.tile_pool(name="lists", bufs=1))
        keep = ctx.enter_context(tc.tile_pool(name="keep", bufs=1))
        reuse = ctx.enter_context(tc.tile_pool(name="reuse", bufs=1))
        psum = ctx.enter_context(tc.psum_pool(name="psum", bufs=1))

        def load_list(source, name):
            tile = lists.tile(list(source.shape), U16, name=name)
            nc.sync.dma_start(tile[:], source)
            return tile

        def load_column(queue, source, name):
            tile = keep.tile([P, PACK], F32, name=name, tag=name, align_bytes=64)
            queue.dma_start(out=tile[:], in_=source.rearrange("(p t) one -> p (t one)", t=PACK))
            return tile

        def load_table_rows(t):
            tile = keep.tile([P, T], F32, name="ta%d" % t, tag="ta%d" % t, align_bytes=64)
            nc.sync.dma_start(out=tile[:], in_=ta.rearrange("(p t) c -> p t c", t=PACK)[:, t, :])
            return tile

        def load_bytes(source, name):
            tile = keep.tile([P, source.shape[1] // 4], I32, name=name, tag=name, align_bytes=64)
            nc.sync.dma_start(out=tile[:], in_=source.bitcast(I32))
            return tile

        def staging(width, first, name):
            tile = keep.tile([P, QUADS, width // 4], I32, name=name)
            nc.vector.memset(tile[first : first + 32, :, :], 0)
            return tile

        def load_scale_rows(queue, staged, first, source):
            rows = source[0].rearrange("(q r) c -> r q c", r=PACK)
            queue.dma_start(out=staged[first : first + PACK, :, :], in_=rows.bitcast(I32))

        def zeroed_plane(width, name):
            plane = keep.tile([P, width], U8, name=name, align_bytes=64)
            nc.vector.memset(plane[:].bitcast(I32), 0)
            return plane

        def load_plane(plane, source):
            rows = source[0].rearrange("(q r) c -> r q c", r=PACK)
            for r in range(PACK):
                nc.sync.dma_start(out=plane[r:P:32, :].bitcast(I32), in_=rows[r].bitcast(I32))

        def spread(staged, first, name):
            plane = keep.tile([P, 4 * staged.shape[2]], U8, name=name, align_bytes=64)
            for q in range(QUADS):
                nc.vector.tensor_copy(
                    out=plane[32 * q : 32 * (q + 1), :].bitcast(I32), in_=staged[first : first + 32, q, :]
                )
            return plane

        def deal(engine_copy, dealt, raw, run):
            engine_copy(
                out=dealt.rearrange("p (t c i) -> p c t i", t=PACK, i=run),
                in_=raw.rearrange("p (c i t) -> p c t i", t=PACK, i=run),
            )

        warm_in = keep.tile([P, 1], F32, name="warm_in")
        warm_out = keep.tile([P, 1], F32, name="warm_out")
        nc.gpsimd.memset(warm_in[:], 0.0)
        nc.scalar.activation(out=warm_out[:], in_=warm_in[:], func=COPY)
        xo_plane = zeroed_plane(M, "xo_plane")
        weight_rows = staging(R, 64, "weight_rows")
        vs_plane = zeroed_plane(S, "vs_plane")

        idx = load_list(offs, "idx")
        ga_sb = load_column(nc.scalar, ga, "ga_sb")
        ta_sb = [load_table_rows(0)]
        gb_sb = load_column(nc.scalar, gb, "gb_sb")
        ta_sb.append(load_table_rows(1))
        idx2 = load_list(offs2, "idx2")
        load_scale_rows(nc.scalar, weight_rows, 64 + PACK, w_scales)
        load_scale_rows(nc.scalar, weight_rows, 64, w2_scales)
        ta_sb.append(load_table_rows(2))
        load_plane(xo_plane, xo_scales)
        idx3 = load_list(offs3, "idx3")
        ta_sb.append(load_table_rows(3))
        w_raw = load_bytes(w_words[0].rearrange("p n t -> p (n t)"), "w_raw")
        load_plane(vs_plane, vs_scales)
        idx7 = load_list(offs7, "idx7")
        xo_raw = reuse.tile([P, M], I32, name="xo_raw", offset=0, align_bytes=64)
        nc.sync.dma_start(out=xo_raw[:], in_=xo_words[0].rearrange("p n t -> p (n t)").bitcast(I32))
        w2_raw = load_bytes(w2_words[0], "w2_raw")
        idx4 = load_list(offs4, "idx4")
        vs_raw = load_bytes(vs_words[0], "vs_raw")
        idx6 = load_list(offs6, "idx6")
        sb_sb = load_column(nc.sync, sb, "sb_sb")
        idx5 = load_list(offs5, "idx5")
        sa_sb = load_column(nc.sync, sa, "sa_sb")

        board = [keep.tile([P, C], F32, name="board%d" % t) for t in range(PACK)]
        for t in range(PACK):
            nc.vector.memset(board[t][:], 0.0)

        xcd = [keep.tile([P, U], F32, name="xcd%d" % t) for t in range(PACK)]

        def spell_words(t):
            nc.scalar.activation(out=xcd[t][:], in_=ta_sb[t][:].indirect(idx[:]), func=COPY, scale=ga_sb[:, t : t + 1])

        def read_slots(h, t, target):
            columns = slice(h * HALF // LIST_ROWS, (h + 1) * HALF // LIST_ROWS)
            nc.scalar.activation(
                out=target, in_=xcd[t][:].indirect(idx2[:, columns]), func=COPY, scale=gb_sb[:, t : t + 1]
            )

        def weave(engine_copy, woven, planes):
            engine_copy(
                out=woven.rearrange("p (c i) t -> p c t i", i=4), in_=planes.rearrange("p t (c i) -> p c t i", i=4)
            )

        planes = keep.tile([P, PACK, HALF], BF16, name="xc0", align_bytes=64)
        spell_words(0)
        spell_words(1)
        read_slots(0, 0, planes[:, 0, :])
        read_slots(0, 1, planes[:, 1, :])
        for t in range(2, PACK):
            spell_words(t)
            read_slots(0, t, planes[:, t, :])

        weight_plane = spread(weight_rows, 64, "weight_plane")
        weight_scale = keep.tile([P, R], U8, name="weight_scale", align_bytes=64)
        deal(nc.vector.tensor_copy, weight_scale[:], weight_plane[:], 16)
        xo_scale = keep.tile([P, J], U8, name="xo_scale", align_bytes=64)
        nc.vector.tensor_copy(out=xo_scale[:], in_=xo_plane[:].indirect(idx3[:]))
        woven = keep.tile([P, HALF, PACK], BF16, name="xc_woven0", align_bytes=64)
        weave(nc.vector.tensor_copy, woven[:, :, 0:2], planes[:, 0:2, :])
        w_codes = keep.tile([P, R], I32, name="w_codes", align_bytes=64)
        deal(nc.vector.tensor_copy, w_codes[:], w_raw[:], 4)
        vs_scale = keep.tile([P, N], U8, name="vs_scale", align_bytes=64)
        nc.vector.tensor_copy(out=vs_scale[:], in_=vs_plane[:].indirect(idx7[:]))

        def shared(shape, dtype, name, tag):
            if tag == "a_first":
                return reuse.tile(shape, dtype, name=name, tag=tag, offset=1024, align_bytes=64)
            return keep.tile(shape, dtype, name=name, tag=tag, align_bytes=64)

        def quantize_slots(h, woven, tag):
            codes = shared([P, HALF], U32, "xc_codes%d" % h, tag)
            scale = keep.tile([P, HALF], U8, name="xc_scale%d" % h, tag="xc_scale%d" % h, align_bytes=64)
            nc.vector.quantize_mx(
                out=codes[:].bitcast(FP8X4), scales=scale[:], in_=woven[:].rearrange("p j t -> p (j t)")
            )
            return codes, scale

        def first_product(h, codes, scale, tiles):
            bank = psum.tile([P, len(tiles), HALF], F32, name="a_bank%d_%d" % (h, tiles[0]), tag="a_bank%d_%d" % (h, tiles[0]))
            for i, t in enumerate(tiles):
                rows = slice(t * P, (t + 1) * P)
                nc.tensor.matmul_mx(
                    out=bank[:, i, :], lhsT=w_codes[:, rows].bitcast(FP8X4), lhsT_scale=weight_scale[PACK:, rows],
                    rhs=codes[:].bitcast(FP8X4), rhs_scale=scale[:], start=True, stop=True,
                )
            return bank

        a_sb = {}

        def empty_bank(h, bank, tiles, tag, pieces):
            tile = shared([P, len(tiles), HALF], F32, "a_sb%d_%d" % (h, tiles[0]), tag)
            for piece in pieces:
                nc.scalar.copy(out=tile[:, piece, :], in_=bank[:, piece, :])
            for i, t in enumerate(tiles):
                a_sb[h, t] = tile[:, i, :]

        def put_on_board(h, t):
            columns = slice(h * HALF // LIST_ROWS, (h + 1) * HALF // LIST_ROWS)
            nc.vector.tensor_copy(out=board[t][:].indirect(idx4[:, columns]), in_=a_sb[h, t])

        weave(nc.vector.tensor_copy, woven[:, :, 2:4], planes[:, 2:4, :])
        codes, scale = quantize_slots(0, woven, "xc_codes0")
        planes = keep.tile([P, PACK, HALF], BF16, name="xc1", tag="ga_sb", align_bytes=64)
        for t in range(PACK):
            read_slots(1, t, planes[:, t, :])
        first_bank = first_product(0, codes, scale, [0])
        rest_bank = first_product(0, codes, scale, [1, 2, 3])
        xo_codes = keep.tile([P, J], U32, name="xo_codes", align_bytes=64)
        nc.vector.tensor_copy(out=xo_codes[:], in_=xo_raw[:].bitcast(U32).indirect(idx3[:]))
        woven = reuse.tile([P, HALF, PACK], BF16, name="xc_woven1", offset=0, align_bytes=64)
        for pair in range(2):
            weave(nc.vector.tensor_copy, woven[:, :, 2 * pair : 2 * pair + 2], planes[:, 2 * pair : 2 * pair + 2, :])
        empty_bank(0, first_bank, [0], "a_first", [slice(0, 1)])
        w2_codes = reuse.tile([P, 2 * R], U8, name="w2_codes", offset=2048, align_bytes=64)
        deal(nc.scalar.copy, w2_codes[:].bitcast(U16), w2_raw[:].bitcast(U16), 8)
        empty_bank(0, rest_bank, [1, 2, 3], "w2_raw", [slice(0, 1), slice(1, 3)])
        put_on_board(0, 0)
        codes, scale = quantize_slots(1, woven, "a_first")
        for t in range(1, PACK):
            put_on_board(0, t)
        empty_bank(1, first_product(1, codes, scale, [0, 1, 2, 3]), [0, 1, 2, 3], "a_second", [slice(0, 4)])

        b_tags = ("a_first", "xc_scale1", "b_sb2", "b_sb3")
        b_sb = [shared([P, J], F32, "b_sb%d" % t, b_tags[t]) for t in range(PACK)]
        from_b = keep.tile([P, PACK, O], F32, name="from_b")
        for pair in range(2):
            bank = psum.tile([P, 2, J], F32, name="b_bank%d" % pair, tag=("b_bank0", "a_bank1_0")[pair])
            for i in range(2):
                t = 2 * pair + i
                nc.tensor.matmul_mx(
                    out=bank[:, i, :], lhsT=w2_codes[:, 2 * t * P : 2 * (t + 1) * P].bitcast(FP4X4),
                    lhsT_scale=weight_scale[:, t * P : (t + 1) * P],
                    rhs=xo_codes[:].bitcast(FP8X4), rhs_scale=xo_scale[:], start=True, stop=True,
                )
            for i in range(2):
                nc.scalar.copy(out=b_sb[2 * pair + i][:], in_=bank[:, i, :])
        for t in range(PACK):
            nc.scalar.activation(
                out=from_b[:, t, :], in_=b_sb[t][:].indirect(idx6[:]), func=COPY, scale=sb_sb[:, t : t + 1]
            )

        from_board = keep.tile([P, PACK, O], F32, name="from_board")
        for t in range(PACK):
            put_on_board(1, t)
            nc.scalar.activation(
                out=from_board[:, t, :], in_=board[t][:].indirect(idx5[:]), func=COPY, scale=sa_sb[:, t : t + 1]
            )

        vs_codes = keep.tile([P, 2 * N], U8, name="vs_codes", tag="a_second", align_bytes=64)
        nc.vector.tensor_copy(out=vs_codes[:].bitcast(U16), in_=vs_raw[:].bitcast(U16).indirect(idx7[:]))
        hid = keep.tile([P, O, PACK], BF16, name="hid", align_bytes=64)
        nc.vector.tensor_tensor(
            out=hid[:].rearrange("p (c i) t -> p c t i", i=4),
            in0=from_board[:].rearrange("p t (c i) -> p c t i", i=4),
            in1=from_b[:].rearrange("p t (c i) -> p c t i", i=4),
            op=MAX,
        )
        hid_codes = keep.tile([P, O], U32, name="hid_codes", align_bytes=64)
        hid_scale = keep.tile([P, O], U8, name="hid_scale", align_bytes=64)
        nc.vector.quantize_mx(
            out=hid_codes[:].bitcast(FP8X4), scales=hid_scale[:], in_=hid[:].rearrange("p o t -> p (o t)")
        )
        for h, (engine_copy, queue) in enumerate(((nc.scalar.copy, nc.scalar), (nc.vector.tensor_copy, nc.sync))):
            bank = psum.tile([P, O], F32, name="y_bank%d" % h)
            nc.tensor.matmul_mx(
                out=bank[:], lhsT=vs_codes[:, 2 * h * P : 2 * (h + 1) * P].bitcast(FP4X4),
                lhsT_scale=vs_scale[:, h * P : (h + 1) * P],
                rhs=hid_codes[:].bitcast(FP8X4), rhs_scale=hid_scale[:], start=True, stop=True,
            )
            result = keep.tile([P, O], F32, name="result%d" % h)
            engine_copy(out=result[:], in_=bank[:])
            queue.dma_start(out=out[h * P : (h + 1) * P, :], in_=result[:])
